import numpy as np
CORES = [34,162,290,418,42,426]
N = 6
TIMES = 2
def setup_inputs(rng):
    x = (rng.standard_normal((N, 128, 128), dtype=np.float32) / np.float32(np.sqrt(512 * N)))
    return {"x": x, "xt": x.transpose(0, 2, 1).copy()}
def setup_inputs_big(rng):
    d = setup_inputs(rng)
    for k in ("x", "xt"): d[k] = (d[k].astype(np.float32) * 1024.0).astype(d[k].dtype)
    return d
def setup_inputs_small(rng):
    d = setup_inputs(rng)
    for k in ("x", "xt"): d[k] = (d[k].astype(np.float32) * (1 / 1024.0)).astype(d[k].dtype)
    return d
def setup_inputs_apart(rng):
    d = setup_inputs(rng)
    f = (10.0 ** rng.permutation(np.linspace(-1.5, 1.5, N))).astype(np.float32).reshape(N, 1, 1)
    for k in ("x", "xt"): d[k] = (d[k].astype(np.float32) * f).astype(d[k].dtype)
    return d
def reference(x, xt):
    X = list(x.astype(np.float64))
    for _ in range(TIMES):
        G = sum(a.T @ a for a in X)
        X = [1.5 * a - 0.5 * (a @ G) for a in X]
    return {"y": np.stack(X).astype(np.float32)}

@@ -1,0 +1,157 @@
+import numpy as np
+from concourse.bass import DstId, RemoteDMATransfer
+from concourse.mybir import dt, AluOpType
+
+D = 128
+H = D // 2
+BANK = 512
+F = "float32"
+
+C_HALF = 0.5
+C_SHIFT = -1.125
+C_T = -0.421875
+C_LIN = -1.078125
+C_ONE = 0.3251953125
+
+SCRATCH = {
+    "xs": ("sbuf", [D, D], F),
+    "xts": ("sbuf", [D, D], F),
+    "xl": ("sbuf", [D, D], F),
+    "ps": ("sbuf", [D, D], F),
+    "pl0": ("sbuf", [D, D], F),
+    "pl1": ("sbuf", [D, D], F),
+    "zd": ("sbuf", [D, D + 1], F),
+    "ed": ("dram", [D + 1, D], F),
+    "idn": ("sbuf", [D, D], F),
+    "half": ("sbuf", [D, D], F),
+    "shI": ("sbuf", [D, D], F),
+    "tI": ("sbuf", [D, D], F),
+    "lxt": ("sbuf", [D, D], F),
+    "ox": ("sbuf", [D, D], F),
+    "gs": ("sbuf", [D, D], F),
+    "t": ("sbuf", [D, D], F),
+    "zt": ("sbuf", [D, D], F),
+    "ysb": ("sbuf", [D, D], F),
+    "pP": ("psum", [D, BANK], F),
+    "pS": ("psum", [D, BANK], F),
+    "pS2": ("psum", [D, BANK], F),
+    "pT": ("psum", [D, BANK], F),
+    "pZ": ("psum", [D, BANK], F),
+    "pY0": ("psum", [D, BANK], F),
+    "pY1": ("psum", [D, BANK], F),
+}
+SEMAPHORES = ["s_x", "s_xt", "s_z0", "s_z", "s_e", "s_i", "s_c", "s_ox", "s_lxt", "s_xl", "s_p", "s_ps", "s_d", "s_s",
+              "s_s2", "s_pl0", "s_pl1", "s_gs", "s_t1", "s_t", "s_z2", "s_zt", "s_y0", "s_y1", "s_y", "s_done", "s_loc"]
+
+
+def _bits(mask):
+    return [b for b in range(mask.bit_length()) if (mask >> b) & 1]
+
+
+def _mask_of(bits):
+    m = 0
+    for b in bits:
+        m |= 1 << b
+    return m
+
+
+def _partner(c, T, topo):
+    return [d for d in T.cores
+            if topo.rack(topo.host(d)) != topo.rack(topo.host(c)) and topo.may_write(c, d) and topo.chip(d) == topo.chip(c)][0]
+
+
+def _peers(c, T, topo):
+    near = [d for d in T.cores if d != c and topo.rack(topo.host(d)) == topo.rack(topo.host(c))]
+    return sorted(near, key=lambda d: (0 if (topo.mates(d, c) or topo.same_plane(d, c)) else 1, T.rank_of(d)))
+
+
+def rank_program(g, core, T, topo):
+    if T.rank_of(core) is None:
+        return
+    S = T.sem
+    pe, ve = g.tensor, g.vector
+    add, mult = AluOpType.add, AluOpType.mult
+    lo, hi = slice(0, H), slice(H, D)
+
+    g.sync.dma_start(T.xs[:], T.x[:]).then_inc(S.s_x, 16)
+    g.scalar.dma_start(T.xts[:], T.xt[:]).then_inc(S.s_xt, 16)
+    ve.memset(T.zd[:], 0.0).then_inc(S.s_z0, 1)
+    ve.wait_ge(S.s_z0, 1)
+    ve.memset(T.zd[:, 0:1], 1.0).then_inc(S.s_z, 1)
+    g.scalar.wait_ge(S.s_z, 1)
+    g.scalar.dma_start(T.ed[:], T.zd[:]).then_inc(S.s_e, 16)
+    g.scalar.wait_ge(S.s_e, 16)
+    g.scalar.dma_start(T.idn[:], T.ed[0:D, :]).then_inc(S.s_i, 16)
+
+    partner = _partner(core, T, topo)
+    peers = _peers(core, T, topo)
+    g.wait_ge(S.s_x, 16)
+    rid, pid = topo.addr(partner, core)
+    m_far = topo.mask(core, partner)
+    g.remote_dma(out_ap=T.xl[:], in_ap=T.xs[:], remote_sem=S.s_xl, local_sem=S.s_loc, pid=pid, routing_id=rid,
+                 dma_engine_mask=m_far)
+    n_far = len(_bits(m_far))
+
+    common = _bits(topo.mask(core, peers[0]) & topo.mask(core, peers[1]))
+    n_near = len(common) // 2
+    trs = []
+    for k, d in enumerate(peers):
+        rid, pid = topo.addr(d, core)
+        slot = _peers(d, T, topo).index(core)
+        trs.append(RemoteDMATransfer(dst_ids=[DstId(rid=rid, pnc=pid)],
+                                     dma_engine_mask=_mask_of(common[k * n_near:(k + 1) * n_near]),
+                                     remote_sem=S["s_pl%d" % slot], src=T.ps[:], dst=T["pl%d" % slot][:]))
+    g.wait_ge(S.s_ps, 1)
+    g.remote_dma_fused(trs, local_sem=S.s_loc)
+    g.wait_ge(S.s_loc, n_far + 2 * n_near)
+
+    for buf, val in ((T.half, C_HALF), (T.shI, C_SHIFT), (T.tI, C_T), (T.lxt, C_LIN), (T.ox, C_ONE)):
+        ve.memset(buf[:], val).then_inc(S.s_c, 1)
+    ve.wait_ge(S.s_c, 5)
+    ve.wait_ge(S.s_x, 16)
+    ve.tensor_tensor(out=T.ox[:], in0=T.ox[:], in1=T.xs[:], op=mult).then_inc(S.s_ox, 1)
+    ve.wait_ge(S.s_xt, 16)
+    ve.tensor_tensor(out=T.lxt[:], in0=T.lxt[:], in1=T.xts[:], op=mult).then_inc(S.s_lxt, 1)
+    ve.wait_ge(S.s_p, 1)
+    ve.tensor_tensor(out=T.ps[:], in0=T.pP[:, 0:D], in1=T.half[:], op=mult).then_inc(S.s_ps, 1)
+    ve.wait_ge(S.s_i, 16)
+    ve.tensor_tensor(out=T.shI[:], in0=T.shI[:], in1=T.idn[:], op=mult).then_inc(S.s_d, 1)
+    ve.tensor_tensor(out=T.tI[:], in0=T.tI[:], in1=T.idn[:], op=mult).then_inc(S.s_d, 1)
+    ve.wait_ge(S.s_d, 2)
+    ve.wait_ge(S.s_ps, 1)
+    ve.tensor_tensor(out=T.pS[:, 0:D], in0=T.ps[:], in1=T.shI[:], op=add).then_inc(S.s_s, 1)
+    ve.wait_ge(S.s_s, 1)
+    ve.wait_ge(S.s_pl0, n_near)
+    ve.tensor_tensor(out=T.pS2[:, 0:D], in0=T.pS[:, 0:D], in1=T.pl0[:], op=add).then_inc(S.s_s2, 1)
+    ve.wait_ge(S.s_s2, 1)
+    ve.wait_ge(S.s_pl1, n_near)
+    ve.tensor_tensor(out=T.gs[:], in0=T.pS2[:, 0:D], in1=T.pl1[:], op=add).then_inc(S.s_gs, 1)
+    ve.wait_ge(S.s_t1, 1)
+    ve.tensor_tensor(out=T.t[:], in0=T.pT[:, 0:D], in1=T.tI[:], op=add).then_inc(S.s_t, 1)
+    ve.wait_ge(S.s_z2, 1)
+    ve.tensor_copy(out=T.zt[:], in_=T.pZ[:, 0:D]).then_inc(S.s_zt, 1)
+    ve.wait_ge(S.s_ox, 1)
+    ve.wait_ge(S.s_y0, 1)
+    ve.tensor_tensor(out=T.ysb[:, lo], in0=T.pY0[:, 0:H], in1=T.ox[:, lo], op=add).then_inc(S.s_y, 1)
+    ve.wait_ge(S.s_y1, 1)
+    ve.tensor_tensor(out=T.ysb[:, hi], in0=T.pY1[:, 0:H], in1=T.ox[:, hi], op=add).then_inc(S.s_y, 1)
+
+    pe.wait_ge(S.s_x, 16)
+    pe.matmul(T.pP[:, 0:D], T.xs[:], T.xs[:], start=True, stop=False)
+    pe.wait_ge(S.s_xl, n_far)
+    pe.matmul(T.pP[:, 0:D], T.xl[:], T.xl[:], start=False, stop=True).then_inc(S.s_p, 1)
+    pe.wait_ge(S.s_xt, 16)
+    pe.wait_ge(S.s_lxt, 1)
+    pe.wait_ge(S.s_gs, 1)
+    pe.matmul(T.pT[:, 0:D], T.gs[:], T.gs[:], start=True, stop=True).then_inc(S.s_t1, 1)
+    pe.matmul(T.pY0[:, 0:H], T.lxt[:], T.gs[:, lo], start=True, stop=False)
+    pe.wait_ge(S.s_t, 1)
+    pe.matmul(T.pZ[:, 0:D], T.t[:], T.xts[:], start=True, stop=True).then_inc(S.s_z2, 1)
+    pe.matmul(T.pY1[:, 0:H], T.lxt[:], T.gs[:, hi], start=True, stop=False)
+    pe.wait_ge(S.s_zt, 1)
+    pe.matmul(T.pY0[:, 0:H], T.zt[:], T.t[:, lo], start=False, stop=True).then_inc(S.s_y0, 1)
+    pe.matmul(T.pY1[:, 0:H], T.zt[:], T.t[:, hi], start=False, stop=True).then_inc(S.s_y1, 1)
+
+    g.sync.wait_ge(S.s_y, 2)
+    g.sync.dma_start(T.y[:], T.ysb[:]).then_inc(S.s_done, 16)
+    g.sync.wait_ge(S.s_done, 16)

@@ -7,41 +7,48 @@ H = D // 2
 BANK = 512
 F = "float32"
 
-C_HALF = 0.5
-C_SHIFT = -1.125
-C_T = -0.421875
-C_LIN = -1.078125
-C_ONE = 0.3251953125
+C_SHIFT = -2.25
+C_T = -1.6875
+C_SQ = 0.0625
+C_LIN = -8.625
+C_ONE = 5.203125
 
 SCRATCH = {
     "xs": ("sbuf", [D, D], F),
     "xts": ("sbuf", [D, D], F),
-    "xl": ("sbuf", [D, D], F),
+    "xr0": ("sbuf", [D, D], F),
+    "xr1": ("sbuf", [D, D], F),
     "ps": ("sbuf", [D, D], F),
-    "pl0": ("sbuf", [D, D], F),
-    "pl1": ("sbuf", [D, D], F),
+    "pl": ("sbuf", [D, D], F),
+    "rl0": ("sbuf", [D, D], F),
+    "rl1": ("sbuf", [D, D], F),
     "zd": ("sbuf", [D, D + 1], F),
     "ed": ("dram", [D + 1, D], F),
     "idn": ("sbuf", [D, D], F),
-    "half": ("sbuf", [D, D], F),
     "shI": ("sbuf", [D, D], F),
     "tI": ("sbuf", [D, D], F),
-    "lxt": ("sbuf", [D, D], F),
-    "ox": ("sbuf", [D, D], F),
+    "oI": ("sbuf", [D, D], F),
+    "cl": ("sbuf", [D, D], F),
+    "qxt": ("sbuf", [D, D], F),
+    "ws": ("sbuf", [D, D], F),
     "gs": ("sbuf", [D, D], F),
     "t": ("sbuf", [D, D], F),
-    "zt": ("sbuf", [D, D], F),
+    "r1": ("sbuf", [D, D], F),
+    "r2": ("sbuf", [D, D], F),
+    "m": ("sbuf", [D, D], F),
     "ysb": ("sbuf", [D, D], F),
     "pP": ("psum", [D, BANK], F),
+    "pR": ("psum", [D, BANK], F),
     "pS": ("psum", [D, BANK], F),
     "pS2": ("psum", [D, BANK], F),
     "pT": ("psum", [D, BANK], F),
-    "pZ": ("psum", [D, BANK], F),
+    "pB": ("psum", [D, BANK], F),
     "pY0": ("psum", [D, BANK], F),
     "pY1": ("psum", [D, BANK], F),
 }
-SEMAPHORES = ["s_x", "s_xt", "s_z0", "s_z", "s_e", "s_i", "s_c", "s_ox", "s_lxt", "s_xl", "s_p", "s_ps", "s_d", "s_s",
-              "s_s2", "s_pl0", "s_pl1", "s_gs", "s_t1", "s_t", "s_z2", "s_zt", "s_y0", "s_y1", "s_y", "s_done", "s_loc"]
+SEMAPHORES = ["s_x", "s_xt", "s_z0", "s_z", "s_e", "s_i", "s_c", "s_qxt", "s_xr0", "s_xr1", "s_p", "s_ps", "s_pl",
+              "s_r", "s_d", "s_w", "s_s", "s_s2", "s_rl0", "s_rl1", "s_gs", "s_t1", "s_t", "s_r1", "s_r2", "s_b", "s_m0",
+              "s_m1", "s_y0", "s_y1", "s_y", "s_done", "s_loc"]
 
 
 def _bits(mask):
@@ -85,72 +92,83 @@ def rank_program(g, core, T, topo):
 
     partner = _partner(core, T, topo)
     peers = _peers(core, T, topo)
+    common = _bits(topo.mask(core, peers[0]) & topo.mask(core, peers[1]) & topo.mask(core, partner))
+    n_half = len(common) // 2
+    first, second = common[:n_half], common[n_half:]
+    n_raw = n_half // 2
+
+    def to_peers(src, name, sem, groups):
+        trs = []
+        for k, d in enumerate(peers):
+            rid, pid = topo.addr(d, core)
+            slot = _peers(d, T, topo).index(core)
+            trs.append(RemoteDMATransfer(dst_ids=[DstId(rid=rid, pnc=pid)], dma_engine_mask=_mask_of(groups[k]),
+                                         remote_sem=S["%s%d" % (sem, slot)], src=src, dst=T["%s%d" % (name, slot)][:]))
+        g.remote_dma_fused(trs, local_sem=S.s_loc)
+
     g.wait_ge(S.s_x, 16)
-    rid, pid = topo.addr(partner, core)
-    m_far = topo.mask(core, partner)
-    g.remote_dma(out_ap=T.xl[:], in_ap=T.xs[:], remote_sem=S.s_xl, local_sem=S.s_loc, pid=pid, routing_id=rid,
-                 dma_engine_mask=m_far)
-    n_far = len(_bits(m_far))
-
-    common = _bits(topo.mask(core, peers[0]) & topo.mask(core, peers[1]))
-    n_near = len(common) // 2
-    trs = []
-    for k, d in enumerate(peers):
-        rid, pid = topo.addr(d, core)
-        slot = _peers(d, T, topo).index(core)
-        trs.append(RemoteDMATransfer(dst_ids=[DstId(rid=rid, pnc=pid)],
-                                     dma_engine_mask=_mask_of(common[k * n_near:(k + 1) * n_near]),
-                                     remote_sem=S["s_pl%d" % slot], src=T.ps[:], dst=T["pl%d" % slot][:]))
+    to_peers(T.xs[:], "xr", "s_xr", [first[:n_raw], first[n_raw:]])
     g.wait_ge(S.s_ps, 1)
-    g.remote_dma_fused(trs, local_sem=S.s_loc)
-    g.wait_ge(S.s_loc, n_far + 2 * n_near)
+    rid, pid = topo.addr(partner, core)
+    g.remote_dma(out_ap=T.pl[:], in_ap=T.ps[:], remote_sem=S.s_pl, local_sem=S.s_loc, pid=pid, routing_id=rid,
+                 dma_engine_mask=_mask_of(second))
+    g.wait_ge(S.s_pl, n_half)
+    to_peers(T.pl[:], "rl", "s_rl", [first, second])
+    g.wait_ge(S.s_loc, 2 * n_raw + n_half + 2 * n_half)
 
-    for buf, val in ((T.half, C_HALF), (T.shI, C_SHIFT), (T.tI, C_T), (T.lxt, C_LIN), (T.ox, C_ONE)):
+    for buf, val in ((T.shI, C_SHIFT), (T.tI, C_T), (T.oI, C_ONE), (T.cl, C_LIN), (T.qxt, C_SQ)):
         ve.memset(buf[:], val).then_inc(S.s_c, 1)
     ve.wait_ge(S.s_c, 5)
-    ve.wait_ge(S.s_x, 16)
-    ve.tensor_tensor(out=T.ox[:], in0=T.ox[:], in1=T.xs[:], op=mult).then_inc(S.s_ox, 1)
-    ve.wait_ge(S.s_xt, 16)
-    ve.tensor_tensor(out=T.lxt[:], in0=T.lxt[:], in1=T.xts[:], op=mult).then_inc(S.s_lxt, 1)
     ve.wait_ge(S.s_p, 1)
-    ve.tensor_tensor(out=T.ps[:], in0=T.pP[:, 0:D], in1=T.half[:], op=mult).then_inc(S.s_ps, 1)
+    ve.tensor_copy(out=T.ps[:], in_=T.pP[:, 0:D]).then_inc(S.s_ps, 1)
+    ve.wait_ge(S.s_xt, 16)
+    ve.tensor_tensor(out=T.qxt[:], in0=T.qxt[:], in1=T.xts[:], op=mult).then_inc(S.s_qxt, 1)
     ve.wait_ge(S.s_i, 16)
-    ve.tensor_tensor(out=T.shI[:], in0=T.shI[:], in1=T.idn[:], op=mult).then_inc(S.s_d, 1)
-    ve.tensor_tensor(out=T.tI[:], in0=T.tI[:], in1=T.idn[:], op=mult).then_inc(S.s_d, 1)
-    ve.wait_ge(S.s_d, 2)
-    ve.wait_ge(S.s_ps, 1)
-    ve.tensor_tensor(out=T.pS[:, 0:D], in0=T.ps[:], in1=T.shI[:], op=add).then_inc(S.s_s, 1)
+    for buf in (T.shI, T.tI, T.oI):
+        ve.tensor_tensor(out=buf[:], in0=buf[:], in1=T.idn[:], op=mult).then_inc(S.s_d, 1)
+    ve.wait_ge(S.s_d, 3)
+    ve.wait_ge(S.s_pl, n_half)
+    ve.tensor_tensor(out=T.ws[:], in0=T.pl[:], in1=T.shI[:], op=add).then_inc(S.s_w, 1)
+    ve.wait_ge(S.s_w, 1)
+    ve.wait_ge(S.s_r, 1)
+    ve.tensor_tensor(out=T.pS[:, 0:D], in0=T.pR[:, 0:D], in1=T.ws[:], op=add).then_inc(S.s_s, 1)
     ve.wait_ge(S.s_s, 1)
-    ve.wait_ge(S.s_pl0, n_near)
-    ve.tensor_tensor(out=T.pS2[:, 0:D], in0=T.pS[:, 0:D], in1=T.pl0[:], op=add).then_inc(S.s_s2, 1)
+    ve.wait_ge(S.s_rl0, n_half)
+    ve.tensor_tensor(out=T.pS2[:, 0:D], in0=T.pS[:, 0:D], in1=T.rl0[:], op=add).then_inc(S.s_s2, 1)
     ve.wait_ge(S.s_s2, 1)
-    ve.wait_ge(S.s_pl1, n_near)
-    ve.tensor_tensor(out=T.gs[:], in0=T.pS2[:, 0:D], in1=T.pl1[:], op=add).then_inc(S.s_gs, 1)
+    ve.wait_ge(S.s_rl1, n_half)
+    ve.tensor_tensor(out=T.gs[:], in0=T.pS2[:, 0:D], in1=T.rl1[:], op=add).then_inc(S.s_gs, 1)
+    ve.wait_ge(S.s_gs, 1)
+    ve.tensor_tensor(out=T.r1[:], in0=T.gs[:], in1=T.cl[:], op=mult).then_inc(S.s_r1, 1)
     ve.wait_ge(S.s_t1, 1)
     ve.tensor_tensor(out=T.t[:], in0=T.pT[:, 0:D], in1=T.tI[:], op=add).then_inc(S.s_t, 1)
-    ve.wait_ge(S.s_z2, 1)
-    ve.tensor_copy(out=T.zt[:], in_=T.pZ[:, 0:D]).then_inc(S.s_zt, 1)
-    ve.wait_ge(S.s_ox, 1)
+    ve.wait_ge(S.s_r1, 1)
+    ve.tensor_tensor(out=T.r2[:], in0=T.r1[:], in1=T.oI[:], op=add).then_inc(S.s_r2, 1)
+    ve.wait_ge(S.s_r2, 1)
+    ve.wait_ge(S.s_b, 1)
+    ve.tensor_tensor(out=T.m[:, lo], in0=T.pB[:, lo], in1=T.r2[:, lo], op=add).then_inc(S.s_m0, 1)
+    ve.tensor_tensor(out=T.m[:, hi], in0=T.pB[:, hi], in1=T.r2[:, hi], op=add).then_inc(S.s_m1, 1)
     ve.wait_ge(S.s_y0, 1)
-    ve.tensor_tensor(out=T.ysb[:, lo], in0=T.pY0[:, 0:H], in1=T.ox[:, lo], op=add).then_inc(S.s_y, 1)
+    ve.tensor_copy(out=T.ysb[:, lo], in_=T.pY0[:, 0:H]).then_inc(S.s_y, 1)
     ve.wait_ge(S.s_y1, 1)
-    ve.tensor_tensor(out=T.ysb[:, hi], in0=T.pY1[:, 0:H], in1=T.ox[:, hi], op=add).then_inc(S.s_y, 1)
+    ve.tensor_copy(out=T.ysb[:, hi], in_=T.pY1[:, 0:H]).then_inc(S.s_y, 1)
 
     pe.wait_ge(S.s_x, 16)
-    pe.matmul(T.pP[:, 0:D], T.xs[:], T.xs[:], start=True, stop=False)
-    pe.wait_ge(S.s_xl, n_far)
-    pe.matmul(T.pP[:, 0:D], T.xl[:], T.xl[:], start=False, stop=True).then_inc(S.s_p, 1)
-    pe.wait_ge(S.s_xt, 16)
-    pe.wait_ge(S.s_lxt, 1)
+    pe.matmul(T.pP[:, 0:D], T.xs[:], T.xs[:], start=True, stop=True).then_inc(S.s_p, 1)
+    pe.matmul(T.pR[:, 0:D], T.xs[:], T.xs[:], start=True, stop=False)
+    pe.wait_ge(S.s_xr0, n_raw)
+    pe.matmul(T.pR[:, 0:D], T.xr0[:], T.xr0[:], start=False, stop=False)
+    pe.wait_ge(S.s_xr1, n_raw)
+    pe.matmul(T.pR[:, 0:D], T.xr1[:], T.xr1[:], start=False, stop=True).then_inc(S.s_r, 1)
+    pe.wait_ge(S.s_qxt, 1)
     pe.wait_ge(S.s_gs, 1)
     pe.matmul(T.pT[:, 0:D], T.gs[:], T.gs[:], start=True, stop=True).then_inc(S.s_t1, 1)
-    pe.matmul(T.pY0[:, 0:H], T.lxt[:], T.gs[:, lo], start=True, stop=False)
     pe.wait_ge(S.s_t, 1)
-    pe.matmul(T.pZ[:, 0:D], T.t[:], T.xts[:], start=True, stop=True).then_inc(S.s_z2, 1)
-    pe.matmul(T.pY1[:, 0:H], T.lxt[:], T.gs[:, hi], start=True, stop=False)
-    pe.wait_ge(S.s_zt, 1)
-    pe.matmul(T.pY0[:, 0:H], T.zt[:], T.t[:, lo], start=False, stop=True).then_inc(S.s_y0, 1)
-    pe.matmul(T.pY1[:, 0:H], T.zt[:], T.t[:, hi], start=False, stop=True).then_inc(S.s_y1, 1)
+    pe.matmul(T.pB[:, 0:D], T.t[:], T.t[:], start=True, stop=True).then_inc(S.s_b, 1)
+    pe.wait_ge(S.s_m0, 1)
+    pe.matmul(T.pY0[:, 0:H], T.qxt[:], T.m[:, lo], start=True, stop=True).then_inc(S.s_y0, 1)
+    pe.wait_ge(S.s_m1, 1)
+    pe.matmul(T.pY1[:, 0:H], T.qxt[:], T.m[:, hi], start=True, stop=True).then_inc(S.s_y1, 1)
 
     g.sync.wait_ge(S.s_y, 2)
     g.sync.dma_start(T.y[:], T.ysb[:]).then_inc(S.s_done, 16)

import numpy as np
from concourse.bass import DstId, RemoteDMATransfer
from concourse.mybir import dt, AluOpType

D = 128
H = D // 2
BANK = 512
F = "float32"

C_SHIFT = -2.25
C_T = -1.6875
C_SQ = 0.0625
C_LIN = -8.625
C_ONE = 5.203125

SCRATCH = {
    "xs": ("sbuf", [D, D], F),
    "xts": ("sbuf", [D, D], F),
    "xr0": ("sbuf", [D, D], F),
    "xr1": ("sbuf", [D, D], F),
    "ps": ("sbuf", [D, D], F),
    "pl": ("sbuf", [D, D], F),
    "rl0": ("sbuf", [D, D], F),
    "rl1": ("sbuf", [D, D], F),
    "zd": ("sbuf", [D, D + 1], F),
    "ed": ("dram", [D + 1, D], F),
    "idn": ("sbuf", [D, D], F),
    "shI": ("sbuf", [D, D], F),
    "tI": ("sbuf", [D, D], F),
    "oI": ("sbuf", [D, D], F),
    "cl": ("sbuf", [D, D], F),
    "qxt": ("sbuf", [D, D], F),
    "ws": ("sbuf", [D, D], F),
    "gs": ("sbuf", [D, D], F),
    "t": ("sbuf", [D, D], F),
    "r1": ("sbuf", [D, D], F),
    "r2": ("sbuf", [D, D], F),
    "m": ("sbuf", [D, D], F),
    "ysb": ("sbuf", [D, D], F),
    "pP": ("psum", [D, BANK], F),
    "pR": ("psum", [D, BANK], F),
    "pS": ("psum", [D, BANK], F),
    "pS2": ("psum", [D, BANK], F),
    "pT": ("psum", [D, BANK], F),
    "pB": ("psum", [D, BANK], F),
    "pY0": ("psum", [D, BANK], F),
    "pY1": ("psum", [D, BANK], F),
}
SEMAPHORES = ["s_x", "s_xt", "s_z0", "s_z", "s_e", "s_i", "s_c", "s_qxt", "s_xr0", "s_xr1", "s_p", "s_ps", "s_pl",
              "s_r", "s_d", "s_w", "s_s", "s_s2", "s_rl0", "s_rl1", "s_gs", "s_t1", "s_t", "s_r1", "s_r2", "s_b", "s_m0",
              "s_m1", "s_y0", "s_y1", "s_y", "s_done", "s_loc"]


def _bits(mask):
    return [b for b in range(mask.bit_length()) if (mask >> b) & 1]


def _mask_of(bits):
    m = 0
    for b in bits:
        m |= 1 << b
    return m


def _partner(c, T, topo):
    return [d for d in T.cores
            if topo.rack(topo.host(d)) != topo.rack(topo.host(c)) and topo.may_write(c, d) and topo.chip(d) == topo.chip(c)][0]


def _peers(c, T, topo):
    near = [d for d in T.cores if d != c and topo.rack(topo.host(d)) == topo.rack(topo.host(c))]
    return sorted(near, key=lambda d: (0 if (topo.mates(d, c) or topo.same_plane(d, c)) else 1, T.rank_of(d)))


def rank_program(g, core, T, topo):
    if T.rank_of(core) is None:
        return
    S = T.sem
    pe, ve = g.tensor, g.vector
    add, mult = AluOpType.add, AluOpType.mult
    lo, hi = slice(0, H), slice(H, D)

    g.sync.dma_start(T.xs[:], T.x[:]).then_inc(S.s_x, 16)
    g.scalar.dma_start(T.xts[:], T.xt[:]).then_inc(S.s_xt, 16)
    ve.memset(T.zd[:], 0.0).then_inc(S.s_z0, 1)
    ve.wait_ge(S.s_z0, 1)
    ve.memset(T.zd[:, 0:1], 1.0).then_inc(S.s_z, 1)
    g.scalar.wait_ge(S.s_z, 1)
    g.scalar.dma_start(T.ed[:], T.zd[:]).then_inc(S.s_e, 16)
    g.scalar.wait_ge(S.s_e, 16)
    g.scalar.dma_start(T.idn[:], T.ed[0:D, :]).then_inc(S.s_i, 16)

    partner = _partner(core, T, topo)
    peers = _peers(core, T, topo)
    common = _bits(topo.mask(core, peers[0]) & topo.mask(core, peers[1]) & topo.mask(core, partner))
    n_half = len(common) // 2
    first, second = common[:n_half], common[n_half:]
    n_raw = n_half // 2

    def to_peers(src, name, sem, groups):
        trs = []
        for k, d in enumerate(peers):
            rid, pid = topo.addr(d, core)
            slot = _peers(d, T, topo).index(core)
            trs.append(RemoteDMATransfer(dst_ids=[DstId(rid=rid, pnc=pid)], dma_engine_mask=_mask_of(groups[k]),
                                         remote_sem=S["%s%d" % (sem, slot)], src=src, dst=T["%s%d" % (name, slot)][:]))
        g.remote_dma_fused(trs, local_sem=S.s_loc)

    g.wait_ge(S.s_x, 16)
    to_peers(T.xs[:], "xr", "s_xr", [first[:n_raw], first[n_raw:]])
    g.wait_ge(S.s_ps, 1)
    rid, pid = topo.addr(partner, core)
    g.remote_dma(out_ap=T.pl[:], in_ap=T.ps[:], remote_sem=S.s_pl, local_sem=S.s_loc, pid=pid, routing_id=rid,
                 dma_engine_mask=_mask_of(second))
    g.wait_ge(S.s_pl, n_half)
    to_peers(T.pl[:], "rl", "s_rl", [first, second])
    g.wait_ge(S.s_loc, 2 * n_raw + n_half + 2 * n_half)

    for buf, val in ((T.shI, C_SHIFT), (T.tI, C_T), (T.oI, C_ONE), (T.cl, C_LIN), (T.qxt, C_SQ)):
        ve.memset(buf[:], val).then_inc(S.s_c, 1)
    ve.wait_ge(S.s_c, 5)
    ve.wait_ge(S.s_p, 1)
    ve.tensor_copy(out=T.ps[:], in_=T.pP[:, 0:D]).then_inc(S.s_ps, 1)
    ve.wait_ge(S.s_xt, 16)
    ve.tensor_tensor(out=T.qxt[:], in0=T.qxt[:], in1=T.xts[:], op=mult).then_inc(S.s_qxt, 1)
    ve.wait_ge(S.s_i, 16)
    for buf in (T.shI, T.tI, T.oI):
        ve.tensor_tensor(out=buf[:], in0=buf[:], in1=T.idn[:], op=mult).then_inc(S.s_d, 1)
    ve.wait_ge(S.s_d, 3)
    ve.wait_ge(S.s_pl, n_half)
    ve.tensor_tensor(out=T.ws[:], in0=T.pl[:], in1=T.shI[:], op=add).then_inc(S.s_w, 1)
    ve.wait_ge(S.s_w, 1)
    ve.wait_ge(S.s_r, 1)
    ve.tensor_tensor(out=T.pS[:, 0:D], in0=T.pR[:, 0:D], in1=T.ws[:], op=add).then_inc(S.s_s, 1)
    ve.wait_ge(S.s_s, 1)
    ve.wait_ge(S.s_rl0, n_half)
    ve.tensor_tensor(out=T.pS2[:, 0:D], in0=T.pS[:, 0:D], in1=T.rl0[:], op=add).then_inc(S.s_s2, 1)
    ve.wait_ge(S.s_s2, 1)
    ve.wait_ge(S.s_rl1, n_half)
    ve.tensor_tensor(out=T.gs[:], in0=T.pS2[:, 0:D], in1=T.rl1[:], op=add).then_inc(S.s_gs, 1)
    ve.wait_ge(S.s_gs, 1)
    ve.tensor_tensor(out=T.r1[:], in0=T.gs[:], in1=T.cl[:], op=mult).then_inc(S.s_r1, 1)
    ve.wait_ge(S.s_t1, 1)
    ve.tensor_tensor(out=T.t[:], in0=T.pT[:, 0:D], in1=T.tI[:], op=add).then_inc(S.s_t, 1)
    ve.wait_ge(S.s_r1, 1)
    ve.tensor_tensor(out=T.r2[:], in0=T.r1[:], in1=T.oI[:], op=add).then_inc(S.s_r2, 1)
    ve.wait_ge(S.s_r2, 1)
    ve.wait_ge(S.s_b, 1)
    ve.tensor_tensor(out=T.m[:, lo], in0=T.pB[:, lo], in1=T.r2[:, lo], op=add).then_inc(S.s_m0, 1)
    ve.tensor_tensor(out=T.m[:, hi], in0=T.pB[:, hi], in1=T.r2[:, hi], op=add).then_inc(S.s_m1, 1)
    ve.wait_ge(S.s_y0, 1)
    ve.tensor_copy(out=T.ysb[:, lo], in_=T.pY0[:, 0:H]).then_inc(S.s_y, 1)
    ve.wait_ge(S.s_y1, 1)
    ve.tensor_copy(out=T.ysb[:, hi], in_=T.pY1[:, 0:H]).then_inc(S.s_y, 1)

    pe.wait_ge(S.s_x, 16)
    pe.matmul(T.pP[:, 0:D], T.xs[:], T.xs[:], start=True, stop=True).then_inc(S.s_p, 1)
    pe.matmul(T.pR[:, 0:D], T.xs[:], T.xs[:], start=True, stop=False)
    pe.wait_ge(S.s_xr0, n_raw)
    pe.matmul(T.pR[:, 0:D], T.xr0[:], T.xr0[:], start=False, stop=False)
    pe.wait_ge(S.s_xr1, n_raw)
    pe.matmul(T.pR[:, 0:D], T.xr1[:], T.xr1[:], start=False, stop=True).then_inc(S.s_r, 1)
    pe.wait_ge(S.s_qxt, 1)
    pe.wait_ge(S.s_gs, 1)
    pe.matmul(T.pT[:, 0:D], T.gs[:], T.gs[:], start=True, stop=True).then_inc(S.s_t1, 1)
    pe.wait_ge(S.s_t, 1)
    pe.matmul(T.pB[:, 0:D], T.t[:], T.t[:], start=True, stop=True).then_inc(S.s_b, 1)
    pe.wait_ge(S.s_m0, 1)
    pe.matmul(T.pY0[:, 0:H], T.qxt[:], T.m[:, lo], start=True, stop=True).then_inc(S.s_y0, 1)
    pe.wait_ge(S.s_m1, 1)
    pe.matmul(T.pY1[:, 0:H], T.qxt[:], T.m[:, hi], start=True, stop=True).then_inc(S.s_y1, 1)

    g.sync.wait_ge(S.s_y, 2)
    g.sync.dma_start(T.y[:], T.ysb[:]).then_inc(S.s_done, 16)
    g.sync.wait_ge(S.s_done, 16)
